import numpy as np, ml_dtypes
CORES = [88,96,104,112,120,216,224,232,240,248]
N = 10
KT, C = 4, 64
B = 2
def setup_inputs(rng):
    return {"x": rng.standard_normal((N, 128, KT * C), dtype=np.float32).astype(ml_dtypes.bfloat16)}
def setup_inputs_big(rng):
    d = setup_inputs(rng)
    for k in ("x",): d[k] = (d[k].astype(np.float32) * 1024.0).astype(d[k].dtype)
    return d
def setup_inputs_small(rng):
    d = setup_inputs(rng)
    for k in ("x",): d[k] = (d[k].astype(np.float32) * (1 / 1024.0)).astype(d[k].dtype)
    return d
def setup_inputs_apart(rng):
    d = setup_inputs(rng)
    f = (10.0 ** rng.permutation(np.linspace(-1.5, 1.5, N))).astype(np.float32).reshape(N, 1, 1)
    for k in ("x",): d[k] = (d[k].astype(np.float32) * f).astype(d[k].dtype)
    return d
def reference(x):
    X = x.astype(np.float64)
    y = np.full((N, C, (2 * B + 1) * C), np.nan)
    for r in range(N):
        for i in range(2 * B + 1):
            s = (r + i - B) % N
            if s != r: y[r][:, C * i:C * i + C] = sum(X[r][:, C * t:C * t + C].T @ X[s][:, C * t:C * t + C] for t in range(KT))
    return {"y": y.astype(ml_dtypes.bfloat16 if x.dtype != np.float64 else np.float64)}

@@ -1,0 +1,147 @@
+from concourse.bass import DstId, RemoteDMATransfer
+
+KT, C, B = 4, 64, 2
+W = KT * C
+NB = 2 * B + 1
+
+SCRATCH = {
+    "xd": ("dram", [128, W], "bfloat16"),
+    "xs": ("sbuf", [128, W], "bfloat16"),
+    "yb": ("sbuf", [128, NB * C], "bfloat16"),
+}
+for _i in range(NB):
+    if _i != B:
+        SCRATCH["land%d" % _i] = ("sbuf", [128, W], "bfloat16")
+        SCRATCH["ps%d" % _i] = ("psum", [128, 512], "float32")
+
+SEMAPHORES = ["ldd", "lds", "harr", "sent", "st"] + ["arr%d" % k for k in range(NB)] \
+    + ["mm%d" % i for i in range(NB) if i != B] + ["cp%d" % i for i in range(NB) if i != B]
+
+_PLAN = {}
+
+
+def _bits(mask):
+    return [b for b in range(mask.bit_length()) if (mask >> b) & 1]
+
+
+def _count(mask):
+    return len(_bits(mask))
+
+
+def _plan(T, topo):
+    if "p" in _PLAN:
+        return _PLAN["p"]
+    cores = list(T.cores)
+    n = len(cores)
+    world = range((max(topo.host(c) for c in cores) + 1) * topo.CORES_PER_HOST)
+    ranks, helpers = [], {}
+    for r, c0 in enumerate(cores):
+        on_chip = [k for k in world if topo.host(k) == topo.host(c0) and topo.chip(k) == topo.chip(c0) and k not in cores]
+        direct, far_away = [], []
+        for j in range(NB):
+            if j == B:
+                continue
+            s = (r + j - B) % n
+            item = (cores[s], NB - 1 - j)
+            (direct if topo.may_write(c0, cores[s]) else far_away).append(item)
+        far_away.sort(key=lambda it: 0 if topo.mates(c0, it[0]) else 1)
+        used, relay = [], []
+        for pos, (d, slot) in enumerate(far_away):
+            owners = [k for k in on_chip if topo.may_write(k, d) and k not in used]
+            near = [k for k in owners if topo.die(k) == topo.die(c0)]
+            far = [k for k in owners if topo.die(k) != topo.die(c0)]
+            h = (near + far)[0] if pos == 0 else (far + near)[0]
+            used.append(h)
+            relay.append((h, d, slot))
+            helpers[h] = (r, d, slot)
+        relay = relay[1:] + relay[:1]
+        ranks.append({"direct": direct, "relay": relay})
+    _PLAN["p"] = (ranks, helpers)
+    return _PLAN["p"]
+
+
+def _dst(topo, d, src):
+    rid, pid = topo.addr(d, src)
+    return DstId(rid=rid, pnc=pid)
+
+
+def rank_program(g, core, T, topo):
+    ranks, helpers = _plan(T, topo)
+    cores = list(T.cores)
+    n = len(cores)
+    rank = T.rank_of(core)
+
+    if rank is None:
+        if core not in helpers:
+            return
+        src_rank, d, slot = helpers[core]
+        c0 = cores[src_rank]
+        off = topo.mask(core, d)
+        rid, pid = topo.addr(d, core)
+        g.wait_ge(T.sem.harr, _count(_onchip_mask(topo, c0, ranks[src_rank])))
+        g.remote_dma(T["land%d" % slot][:], T.xd[:], T.sem["arr%d" % (src_rank % NB)], T.sem.sent, pid, rid, off)
+        g.wait_ge(T.sem.sent, _count(off))
+        return
+
+    me = ranks[rank]
+    g.sync.dma_start(T.xd[:], T.x[:]).then_inc(T.sem.ldd, 16)
+    g.scalar.dma_start(T.xs[:], T.x[:]).then_inc(T.sem.lds, 16)
+
+    g.wait_ge(T.sem.ldd, 16)
+    sent = 0
+    on = _onchip_mask(topo, core, me)
+    g.remote_dma_fused([RemoteDMATransfer(
+        dst_ids=[_dst(topo, h, core) for h, _, _ in me["relay"]], dma_engine_mask=on, remote_sem=T.sem.harr,
+        srcs=[T.xd[:]], dsts=[T.xd[:] for _ in me["relay"]], alu_op=0)], local_sem=T.sem.sent)
+    sent += _count(on)
+    off = _offchip_mask(topo, core, me)
+    g.remote_dma_fused([RemoteDMATransfer(
+        dst_ids=[_dst(topo, d, core) for d, _ in me["direct"]], dma_engine_mask=off, remote_sem=T.sem["arr%d" % (rank % NB)],
+        srcs=[T.xd[:]], dsts=[T["land%d" % slot][:] for _, slot in me["direct"]], alu_op=0)], local_sem=T.sem.sent)
+    sent += _count(off)
+
+    order = []
+    for i in range(NB):
+        if i == B:
+            continue
+        q = (rank + i - B) % n
+        them = ranks[q]
+        if any(d == core for d, _ in them["direct"]):
+            when, cnt = 0, _count(_offchip_mask(topo, cores[q], them))
+        else:
+            pos = [k for k, (_, d, _) in enumerate(them["relay"]) if d == core][0]
+            when, cnt = 1 + pos, _count(topo.mask(them["relay"][pos][0], core))
+        order.append((when, i, q, cnt))
+    order.sort()
+
+    g.tensor.wait_ge(T.sem.lds, 16)
+    stores = [g.sync, g.scalar]
+    for k, (_, i, q, cnt) in enumerate(order):
+        land, ps = T["land%d" % i], T["ps%d" % i]
+        g.tensor.wait_ge(T.sem["arr%d" % (q % NB)], cnt)
+        for t in range(KT):
+            mm = g.tensor.matmul(ps[0:C, 0:C], T.xs[:, C * t:C * t + C], land[:, C * t:C * t + C],
+                                 start=(t == 0), stop=(t == KT - 1))
+        mm.then_inc(T.sem["mm%d" % i], 1)
+        g.vector.wait_ge(T.sem["mm%d" % i], 1)
+        g.vector.tensor_copy(T.yb[0:C, C * i:C * i + C], ps[0:C, 0:C]).then_inc(T.sem["cp%d" % i], 1)
+        sq = stores[k % 2]
+        sq.wait_ge(T.sem["cp%d" % i], 1)
+        sq.dma_start(T.y[:, C * i:C * i + C], T.yb[0:C, C * i:C * i + C]).then_inc(T.sem.st, 16)
+
+    g.wait_ge(T.sem.sent, sent)
+    g.wait_ge(T.sem.st, 16 * len(order))
+
+
+def _offchip_mask(topo, c0, me):
+    m = -1
+    for d, _ in me["direct"]:
+        m &= topo.mask(c0, d)
+    return m
+
+
+def _onchip_mask(topo, c0, me):
+    m = -1
+    for h, _, _ in me["relay"]:
+        m &= topo.mask(c0, h)
+    return m & ~_offchip_mask(topo, c0, me)

@@ -3,10 +3,12 @@ from concourse.bass import DstId, RemoteDMATransfer
 KT, C, B = 4, 64, 2
 W = KT * C
 NB = 2 * B + 1
+RA = 128 * C // W
 
 SCRATCH = {
-    "xd": ("dram", [128, W], "bfloat16"),
-    "xs": ("sbuf", [128, W], "bfloat16"),
+    "xa": ("dram", [128, C], "bfloat16"),
+    "xb": ("dram", [128, W - C], "bfloat16"),
+    "xp": ("sbuf", [128, W], "bfloat16"),
     "yb": ("sbuf", [128, NB * C], "bfloat16"),
 }
 for _i in range(NB):
@@ -14,18 +16,15 @@ for _i in range(NB):
         SCRATCH["land%d" % _i] = ("sbuf", [128, W], "bfloat16")
         SCRATCH["ps%d" % _i] = ("psum", [128, 512], "float32")
 
-SEMAPHORES = ["ldd", "lds", "harr", "sent", "st"] + ["arr%d" % k for k in range(NB)] \
+SEMAPHORES = ["lda", "ldb", "ldp", "harra", "harrb", "sent", "st"] \
+    + ["arr%d" % k for k in range(NB)] + ["ara%d" % k for k in range(NB)] \
     + ["mm%d" % i for i in range(NB) if i != B] + ["cp%d" % i for i in range(NB) if i != B]
 
 _PLAN = {}
 
 
-def _bits(mask):
-    return [b for b in range(mask.bit_length()) if (mask >> b) & 1]
-
-
 def _count(mask):
-    return len(_bits(mask))
+    return len([b for b in range(mask.bit_length()) if (mask >> b) & 1])
 
 
 def _plan(T, topo):
@@ -65,74 +64,6 @@ def _dst(topo, d, src):
     return DstId(rid=rid, pnc=pid)
 
 
-def rank_program(g, core, T, topo):
-    ranks, helpers = _plan(T, topo)
-    cores = list(T.cores)
-    n = len(cores)
-    rank = T.rank_of(core)
-
-    if rank is None:
-        if core not in helpers:
-            return
-        src_rank, d, slot = helpers[core]
-        c0 = cores[src_rank]
-        off = topo.mask(core, d)
-        rid, pid = topo.addr(d, core)
-        g.wait_ge(T.sem.harr, _count(_onchip_mask(topo, c0, ranks[src_rank])))
-        g.remote_dma(T["land%d" % slot][:], T.xd[:], T.sem["arr%d" % (src_rank % NB)], T.sem.sent, pid, rid, off)
-        g.wait_ge(T.sem.sent, _count(off))
-        return
-
-    me = ranks[rank]
-    g.sync.dma_start(T.xd[:], T.x[:]).then_inc(T.sem.ldd, 16)
-    g.scalar.dma_start(T.xs[:], T.x[:]).then_inc(T.sem.lds, 16)
-
-    g.wait_ge(T.sem.ldd, 16)
-    sent = 0
-    on = _onchip_mask(topo, core, me)
-    g.remote_dma_fused([RemoteDMATransfer(
-        dst_ids=[_dst(topo, h, core) for h, _, _ in me["relay"]], dma_engine_mask=on, remote_sem=T.sem.harr,
-        srcs=[T.xd[:]], dsts=[T.xd[:] for _ in me["relay"]], alu_op=0)], local_sem=T.sem.sent)
-    sent += _count(on)
-    off = _offchip_mask(topo, core, me)
-    g.remote_dma_fused([RemoteDMATransfer(
-        dst_ids=[_dst(topo, d, core) for d, _ in me["direct"]], dma_engine_mask=off, remote_sem=T.sem["arr%d" % (rank % NB)],
-        srcs=[T.xd[:]], dsts=[T["land%d" % slot][:] for _, slot in me["direct"]], alu_op=0)], local_sem=T.sem.sent)
-    sent += _count(off)
-
-    order = []
-    for i in range(NB):
-        if i == B:
-            continue
-        q = (rank + i - B) % n
-        them = ranks[q]
-        if any(d == core for d, _ in them["direct"]):
-            when, cnt = 0, _count(_offchip_mask(topo, cores[q], them))
-        else:
-            pos = [k for k, (_, d, _) in enumerate(them["relay"]) if d == core][0]
-            when, cnt = 1 + pos, _count(topo.mask(them["relay"][pos][0], core))
-        order.append((when, i, q, cnt))
-    order.sort()
-
-    g.tensor.wait_ge(T.sem.lds, 16)
-    stores = [g.sync, g.scalar]
-    for k, (_, i, q, cnt) in enumerate(order):
-        land, ps = T["land%d" % i], T["ps%d" % i]
-        g.tensor.wait_ge(T.sem["arr%d" % (q % NB)], cnt)
-        for t in range(KT):
-            mm = g.tensor.matmul(ps[0:C, 0:C], T.xs[:, C * t:C * t + C], land[:, C * t:C * t + C],
-                                 start=(t == 0), stop=(t == KT - 1))
-        mm.then_inc(T.sem["mm%d" % i], 1)
-        g.vector.wait_ge(T.sem["mm%d" % i], 1)
-        g.vector.tensor_copy(T.yb[0:C, C * i:C * i + C], ps[0:C, 0:C]).then_inc(T.sem["cp%d" % i], 1)
-        sq = stores[k % 2]
-        sq.wait_ge(T.sem["cp%d" % i], 1)
-        sq.dma_start(T.y[:, C * i:C * i + C], T.yb[0:C, C * i:C * i + C]).then_inc(T.sem.st, 16)
-
-    g.wait_ge(T.sem.sent, sent)
-    g.wait_ge(T.sem.st, 16 * len(order))
-
-
 def _offchip_mask(topo, c0, me):
     m = -1
     for d, _ in me["direct"]:
@@ -145,3 +76,95 @@ def _onchip_mask(topo, c0, me):
     for h, _, _ in me["relay"]:
         m &= topo.mask(c0, h)
     return m & ~_offchip_mask(topo, c0, me)
+
+
+def rank_program(g, core, T, topo):
+    ranks, helpers = _plan(T, topo)
+    cores = list(T.cores)
+    n = len(cores)
+    rank = T.rank_of(core)
+
+    if rank is None:
+        if core not in helpers:
+            return
+        src_rank, d, slot = helpers[core]
+        on = _count(_onchip_mask(topo, cores[src_rank], ranks[src_rank]))
+        off = topo.mask(core, d)
+        rid, pid = topo.addr(d, core)
+        land = T["land%d" % slot]
+        g.wait_ge(T.sem.harra, on)
+        g.remote_dma(land[:, 0:C], T.xa[:], T.sem["ara%d" % (src_rank % NB)], T.sem.sent, pid, rid, off)
+        g.wait_ge(T.sem.harrb, on)
+        g.remote_dma(land[:, C:W], T.xb[:], T.sem["arr%d" % (src_rank % NB)], T.sem.sent, pid, rid, off)
+        g.wait_ge(T.sem.sent, 2 * _count(off))
+        return
+
+    me = ranks[rank]
+    g.sync.dma_start(T.xa[:], T.x[0:RA, :]).then_inc(T.sem.lda, 16)
+    g.scalar.dma_start(T.xb[:], T.x[RA:128, :]).then_inc(T.sem.ldb, 16)
+    g.sync.dma_start(T.xp[:, 0:C], T.x[0:RA, :]).then_inc(T.sem.ldp, 16)
+    g.scalar.dma_start(T.xp[:, C:W], T.x[RA:128, :]).then_inc(T.sem.ldp, 16)
+
+    sent = 0
+    on = _onchip_mask(topo, core, me)
+    for ld, buf, sem in ((T.sem.lda, T.xa, T.sem.harra), (T.sem.ldb, T.xb, T.sem.harrb)):
+        g.wait_ge(ld, 16)
+        g.remote_dma_fused([RemoteDMATransfer(
+            dst_ids=[_dst(topo, h, core) for h, _, _ in me["relay"]], dma_engine_mask=on, remote_sem=sem,
+            srcs=[buf[:]], dsts=[buf[:] for _ in me["relay"]], alu_op=0)], local_sem=T.sem.sent)
+        sent += _count(on)
+    off = _offchip_mask(topo, core, me)
+    g.wait_ge(T.sem.ldp, 32)
+    g.remote_dma_fused([RemoteDMATransfer(
+        dst_ids=[_dst(topo, d, core) for d, _ in me["direct"]], dma_engine_mask=off, remote_sem=T.sem["arr%d" % (rank % NB)],
+        srcs=[T.xp[:]], dsts=[T["land%d" % slot][:] for _, slot in me["direct"]], alu_op=0)], local_sem=T.sem.sent)
+    sent += _count(off)
+
+    straight, relayed = [], []
+    for i in range(NB):
+        if i == B:
+            continue
+        q = (rank + i - B) % n
+        them = ranks[q]
+        if any(d == core for d, _ in them["direct"]):
+            pos = [k for k, (d, _) in enumerate(them["direct"]) if d == core][0]
+            straight.append((pos, i, q, _count(_offchip_mask(topo, cores[q], them))))
+        else:
+            pos = [k for k, (_, d, _) in enumerate(them["relay"]) if d == core][0]
+            relayed.append((pos, i, q, _count(topo.mask(them["relay"][pos][0], core))))
+    straight.sort()
+    relayed.sort()
+
+    stores = [g.sync, g.scalar]
+    done = [0]
+
+    def finish(mm, i):
+        mm.then_inc(T.sem["mm%d" % i], 1)
+        g.vector.wait_ge(T.sem["mm%d" % i], 1)
+        g.vector.tensor_copy(T.yb[0:C, C * i:C * i + C], T["ps%d" % i][0:C, 0:C]).then_inc(T.sem["cp%d" % i], 1)
+        sq = stores[done[0] % 2]
+        sq.wait_ge(T.sem["cp%d" % i], 1)
+        sq.dma_start(T.y[:, C * i:C * i + C], T.yb[0:C, C * i:C * i + C]).then_inc(T.sem.st, 16)
+        done[0] += 1
+
+    def mult(i, t):
+        return g.tensor.matmul(T["ps%d" % i][0:C, 0:C], T.xp[:, C * t:C * t + C], T["land%d" % i][:, C * t:C * t + C],
+                               start=(t == 0), stop=(t == KT - 1))
+
+    g.tensor.wait_ge(T.sem.ldp, 32)
+    for _, i, q, cnt in straight:
+        g.tensor.wait_ge(T.sem["arr%d" % (q % NB)], cnt)
+        for t in range(KT):
+            mm = mult(i, t)
+        finish(mm, i)
+    for _, i, q, cnt in relayed:
+        g.tensor.wait_ge(T.sem["ara%d" % (q % NB)], cnt)
+        mult(i, 0)
+    for _, i, q, cnt in relayed:
+        g.tensor.wait_ge(T.sem["arr%d" % (q % NB)], cnt)
+        for t in range(1, KT):
+            mm = mult(i, t)
+        finish(mm, i)
+
+    g.wait_ge(T.sem.sent, sent)
+    g.wait_ge(T.sem.st, 16 * done[0])

@@ -4,6 +4,7 @@ KT, C, B = 4, 64, 2
 W = KT * C
 NB = 2 * B + 1
 RA = 128 * C // W
+MAIN = 2
 
 SCRATCH = {
     "xa": ("dram", [128, C], "bfloat16"),
@@ -33,28 +34,64 @@ def _plan(T, topo):
     cores = list(T.cores)
     n = len(cores)
     world = range((max(topo.host(c) for c in cores) + 1) * topo.CORES_PER_HOST)
-    ranks, helpers = [], {}
+    direct, copies, owners = [], [], []
     for r, c0 in enumerate(cores):
-        on_chip = [k for k in world if topo.host(k) == topo.host(c0) and topo.chip(k) == topo.chip(c0) and k not in cores]
-        direct, far_away = [], []
+        direct.append([])
         for j in range(NB):
             if j == B:
                 continue
             s = (r + j - B) % n
-            item = (cores[s], NB - 1 - j)
-            (direct if topo.may_write(c0, cores[s]) else far_away).append(item)
-        far_away.sort(key=lambda it: 0 if topo.mates(c0, it[0]) else 1)
+            if topo.may_write(c0, cores[s]):
+                direct[r].append((cores[s], NB - 1 - j))
+            else:
+                copies.append((r, cores[s], NB - 1 - j))
+        owners.append([k for k in world if topo.host(k) == topo.host(c0) and topo.chip(k) == topo.chip(c0) and k not in cores
+                       and all(topo.may_write(k, d) for q, d, _ in copies if q == r)])
+    dies = sorted(set(topo.die(k) for own in owners for k in own))
+
+    def straight_in(d, die):
+        return len([1 for q in range(n) for e, _ in direct[q] if e == d and topo.die(cores[q]) == die])
+
+    def straight_out(c0, die):
+        return sum(len(direct[q]) for q in range(n) if topo.mates(cores[q], c0) and topo.die(cores[q]) == die)
+
+    best = [None]
+
+    def search(i, asg, load):
+        if i == len(copies):
+            shared = len([1 for k, v in load.items() if k[0] == "mate" and v > 1])
+            across = len([1 for (r, _, _), die in zip(copies, asg) if die != topo.die(cores[r])])
+            meets = sum(straight_in(d, die) + straight_out(cores[r], die)
+                        for (r, d, _), die in zip(copies, asg) if not topo.mates(cores[r], d))
+            key = (shared, across, meets, tuple(asg))
+            if best[0] is None or key < best[0]:
+                best[0] = key
+            return
+        r, d, _ = copies[i]
+        for die in dies:
+            ports = [(("mate", r, die), len([k for k in owners[r] if topo.die(k) == die]))]
+            if not topo.mates(cores[r], d):
+                ports += [(("out", r, die), 1), (("in", d, die), 1)]
+            if any(load.get(p, 0) >= cap for p, cap in ports):
+                continue
+            for p, _ in ports:
+                load[p] = load.get(p, 0) + 1
+            search(i + 1, asg + [die], load)
+            for p, _ in ports:
+                load[p] -= 1
+
+    search(0, [], {})
+    ranks, helpers = [], {}
+    for r, c0 in enumerate(cores):
+        mine = [(d, slot, die) for (q, d, slot), die in zip(copies, best[0][3]) if q == r]
+        mine.sort(key=lambda it: (1 if topo.mates(c0, it[0]) else 0, 1 if it[2] == topo.die(c0) else 0))
         used, relay = [], []
-        for pos, (d, slot) in enumerate(far_away):
-            owners = [k for k in on_chip if topo.may_write(k, d) and k not in used]
-            near = [k for k in owners if topo.die(k) == topo.die(c0)]
-            far = [k for k in owners if topo.die(k) != topo.die(c0)]
-            h = (near + far)[0] if pos == 0 else (far + near)[0]
+        for d, slot, die in mine:
+            h = [k for k in owners[r] if topo.die(k) == die and k not in used][0]
             used.append(h)
+            helpers[h] = (r, d, slot, len(relay))
             relay.append((h, d, slot))
-            helpers[h] = (r, d, slot)
-        relay = relay[1:] + relay[:1]
-        ranks.append({"direct": direct, "relay": relay})
+        ranks.append({"direct": direct[r], "relay": relay})
     _PLAN["p"] = (ranks, helpers)
     return _PLAN["p"]
 
@@ -87,14 +124,15 @@ def rank_program(g, core, T, topo):
     if rank is None:
         if core not in helpers:
             return
-        src_rank, d, slot = helpers[core]
+        src_rank, d, slot, place = helpers[core]
         on = _count(_onchip_mask(topo, cores[src_rank], ranks[src_rank]))
+        onb = on if place < MAIN else _count(_offchip_mask(topo, cores[src_rank], ranks[src_rank]))
         off = topo.mask(core, d)
         rid, pid = topo.addr(d, core)
         land = T["land%d" % slot]
         g.wait_ge(T.sem.harra, on)
         g.remote_dma(land[:, 0:C], T.xa[:], T.sem["ara%d" % (src_rank % NB)], T.sem.sent, pid, rid, off)
-        g.wait_ge(T.sem.harrb, on)
+        g.wait_ge(T.sem.harrb, onb)
         g.remote_dma(land[:, C:W], T.xb[:], T.sem["arr%d" % (src_rank % NB)], T.sem.sent, pid, rid, off)
         g.wait_ge(T.sem.sent, 2 * _count(off))
         return
@@ -105,20 +143,27 @@ def rank_program(g, core, T, topo):
     g.sync.dma_start(T.xp[:, 0:C], T.x[0:RA, :]).then_inc(T.sem.ldp, 16)
     g.scalar.dma_start(T.xp[:, C:W], T.x[RA:128, :]).then_inc(T.sem.ldp, 16)
 
-    sent = 0
+    sent = [0]
     on = _onchip_mask(topo, core, me)
-    for ld, buf, sem in ((T.sem.lda, T.xa, T.sem.harra), (T.sem.ldb, T.xb, T.sem.harrb)):
-        g.wait_ge(ld, 16)
-        g.remote_dma_fused([RemoteDMATransfer(
-            dst_ids=[_dst(topo, h, core) for h, _, _ in me["relay"]], dma_engine_mask=on, remote_sem=sem,
-            srcs=[buf[:]], dsts=[buf[:] for _ in me["relay"]], alu_op=0)], local_sem=T.sem.sent)
-        sent += _count(on)
     off = _offchip_mask(topo, core, me)
+
+    def on_chip(buf, sem, who, mask):
+        g.remote_dma_fused([RemoteDMATransfer(
+            dst_ids=[_dst(topo, h, core) for h, _, _ in who], dma_engine_mask=mask, remote_sem=sem,
+            srcs=[buf[:]], dsts=[buf[:] for _ in who], alu_op=0)], local_sem=T.sem.sent)
+        sent[0] += _count(mask)
+
+    g.wait_ge(T.sem.lda, 16)
+    on_chip(T.xa, T.sem.harra, me["relay"], on)
+    g.wait_ge(T.sem.ldb, 16)
+    on_chip(T.xb, T.sem.harrb, me["relay"][:MAIN], on)
+    if me["relay"][MAIN:]:
+        on_chip(T.xb, T.sem.harrb, me["relay"][MAIN:], off)
     g.wait_ge(T.sem.ldp, 32)
     g.remote_dma_fused([RemoteDMATransfer(
         dst_ids=[_dst(topo, d, core) for d, _ in me["direct"]], dma_engine_mask=off, remote_sem=T.sem["arr%d" % (rank % NB)],
         srcs=[T.xp[:]], dsts=[T["land%d" % slot][:] for _, slot in me["direct"]], alu_op=0)], local_sem=T.sem.sent)
-    sent += _count(off)
+    sent[0] += _count(off)
 
     straight, relayed = [], []
     for i in range(NB):
@@ -166,5 +211,5 @@ def rank_program(g, core, T, topo):
             mm = mult(i, t)
         finish(mm, i)
 
-    g.wait_ge(T.sem.sent, sent)
+    g.wait_ge(T.sem.sent, sent[0])
     g.wait_ge(T.sem.st, 16 * done[0])

from concourse.bass import DstId, RemoteDMATransfer

KT, C, B = 4, 64, 2
W = KT * C
NB = 2 * B + 1
RA = 128 * C // W
MAIN = 2

SCRATCH = {
    "xa": ("dram", [128, C], "bfloat16"),
    "xb": ("dram", [128, W - C], "bfloat16"),
    "xp": ("sbuf", [128, W], "bfloat16"),
    "yb": ("sbuf", [128, NB * C], "bfloat16"),
}
for _i in range(NB):
    if _i != B:
        SCRATCH["land%d" % _i] = ("sbuf", [128, W], "bfloat16")
        SCRATCH["ps%d" % _i] = ("psum", [128, 512], "float32")

SEMAPHORES = ["lda", "ldb", "ldp", "harra", "harrb", "sent", "st"] \
    + ["arr%d" % k for k in range(NB)] + ["ara%d" % k for k in range(NB)] \
    + ["mm%d" % i for i in range(NB) if i != B] + ["cp%d" % i for i in range(NB) if i != B]

_PLAN = {}


def _count(mask):
    return len([b for b in range(mask.bit_length()) if (mask >> b) & 1])


def _plan(T, topo):
    if "p" in _PLAN:
        return _PLAN["p"]
    cores = list(T.cores)
    n = len(cores)
    world = range((max(topo.host(c) for c in cores) + 1) * topo.CORES_PER_HOST)
    direct, copies, owners = [], [], []
    for r, c0 in enumerate(cores):
        direct.append([])
        for j in range(NB):
            if j == B:
                continue
            s = (r + j - B) % n
            if topo.may_write(c0, cores[s]):
                direct[r].append((cores[s], NB - 1 - j))
            else:
                copies.append((r, cores[s], NB - 1 - j))
        owners.append([k for k in world if topo.host(k) == topo.host(c0) and topo.chip(k) == topo.chip(c0) and k not in cores
                       and all(topo.may_write(k, d) for q, d, _ in copies if q == r)])
    dies = sorted(set(topo.die(k) for own in owners for k in own))

    def straight_in(d, die):
        return len([1 for q in range(n) for e, _ in direct[q] if e == d and topo.die(cores[q]) == die])

    def straight_out(c0, die):
        return sum(len(direct[q]) for q in range(n) if topo.mates(cores[q], c0) and topo.die(cores[q]) == die)

    best = [None]

    def search(i, asg, load):
        if i == len(copies):
            shared = len([1 for k, v in load.items() if k[0] == "mate" and v > 1])
            across = len([1 for (r, _, _), die in zip(copies, asg) if die != topo.die(cores[r])])
            meets = sum(straight_in(d, die) + straight_out(cores[r], die)
                        for (r, d, _), die in zip(copies, asg) if not topo.mates(cores[r], d))
            key = (shared, across, meets, tuple(asg))
            if best[0] is None or key < best[0]:
                best[0] = key
            return
        r, d, _ = copies[i]
        for die in dies:
            ports = [(("mate", r, die), len([k for k in owners[r] if topo.die(k) == die]))]
            if not topo.mates(cores[r], d):
                ports += [(("out", r, die), 1), (("in", d, die), 1)]
            if any(load.get(p, 0) >= cap for p, cap in ports):
                continue
            for p, _ in ports:
                load[p] = load.get(p, 0) + 1
            search(i + 1, asg + [die], load)
            for p, _ in ports:
                load[p] -= 1

    search(0, [], {})
    ranks, helpers = [], {}
    for r, c0 in enumerate(cores):
        mine = [(d, slot, die) for (q, d, slot), die in zip(copies, best[0][3]) if q == r]
        mine.sort(key=lambda it: (1 if topo.mates(c0, it[0]) else 0, 1 if it[2] == topo.die(c0) else 0))
        used, relay = [], []
        for d, slot, die in mine:
            h = [k for k in owners[r] if topo.die(k) == die and k not in used][0]
            used.append(h)
            helpers[h] = (r, d, slot, len(relay))
            relay.append((h, d, slot))
        ranks.append({"direct": direct[r], "relay": relay})
    _PLAN["p"] = (ranks, helpers)
    return _PLAN["p"]


def _dst(topo, d, src):
    rid, pid = topo.addr(d, src)
    return DstId(rid=rid, pnc=pid)


def _offchip_mask(topo, c0, me):
    m = -1
    for d, _ in me["direct"]:
        m &= topo.mask(c0, d)
    return m


def _onchip_mask(topo, c0, me):
    m = -1
    for h, _, _ in me["relay"]:
        m &= topo.mask(c0, h)
    return m & ~_offchip_mask(topo, c0, me)


def rank_program(g, core, T, topo):
    ranks, helpers = _plan(T, topo)
    cores = list(T.cores)
    n = len(cores)
    rank = T.rank_of(core)

    if rank is None:
        if core not in helpers:
            return
        src_rank, d, slot, place = helpers[core]
        on = _count(_onchip_mask(topo, cores[src_rank], ranks[src_rank]))
        onb = on if place < MAIN else _count(_offchip_mask(topo, cores[src_rank], ranks[src_rank]))
        off = topo.mask(core, d)
        rid, pid = topo.addr(d, core)
        land = T["land%d" % slot]
        g.wait_ge(T.sem.harra, on)
        g.remote_dma(land[:, 0:C], T.xa[:], T.sem["ara%d" % (src_rank % NB)], T.sem.sent, pid, rid, off)
        g.wait_ge(T.sem.harrb, onb)
        g.remote_dma(land[:, C:W], T.xb[:], T.sem["arr%d" % (src_rank % NB)], T.sem.sent, pid, rid, off)
        g.wait_ge(T.sem.sent, 2 * _count(off))
        return

    me = ranks[rank]
    g.sync.dma_start(T.xa[:], T.x[0:RA, :]).then_inc(T.sem.lda, 16)
    g.scalar.dma_start(T.xb[:], T.x[RA:128, :]).then_inc(T.sem.ldb, 16)
    g.sync.dma_start(T.xp[:, 0:C], T.x[0:RA, :]).then_inc(T.sem.ldp, 16)
    g.scalar.dma_start(T.xp[:, C:W], T.x[RA:128, :]).then_inc(T.sem.ldp, 16)

    sent = [0]
    on = _onchip_mask(topo, core, me)
    off = _offchip_mask(topo, core, me)

    def on_chip(buf, sem, who, mask):
        g.remote_dma_fused([RemoteDMATransfer(
            dst_ids=[_dst(topo, h, core) for h, _, _ in who], dma_engine_mask=mask, remote_sem=sem,
            srcs=[buf[:]], dsts=[buf[:] for _ in who], alu_op=0)], local_sem=T.sem.sent)
        sent[0] += _count(mask)

    g.wait_ge(T.sem.lda, 16)
    on_chip(T.xa, T.sem.harra, me["relay"], on)
    g.wait_ge(T.sem.ldb, 16)
    on_chip(T.xb, T.sem.harrb, me["relay"][:MAIN], on)
    if me["relay"][MAIN:]:
        on_chip(T.xb, T.sem.harrb, me["relay"][MAIN:], off)
    g.wait_ge(T.sem.ldp, 32)
    g.remote_dma_fused([RemoteDMATransfer(
        dst_ids=[_dst(topo, d, core) for d, _ in me["direct"]], dma_engine_mask=off, remote_sem=T.sem["arr%d" % (rank % NB)],
        srcs=[T.xp[:]], dsts=[T["land%d" % slot][:] for _, slot in me["direct"]], alu_op=0)], local_sem=T.sem.sent)
    sent[0] += _count(off)

    straight, relayed = [], []
    for i in range(NB):
        if i == B:
            continue
        q = (rank + i - B) % n
        them = ranks[q]
        if any(d == core for d, _ in them["direct"]):
            pos = [k for k, (d, _) in enumerate(them["direct"]) if d == core][0]
            straight.append((pos, i, q, _count(_offchip_mask(topo, cores[q], them))))
        else:
            pos = [k for k, (_, d, _) in enumerate(them["relay"]) if d == core][0]
            relayed.append((pos, i, q, _count(topo.mask(them["relay"][pos][0], core))))
    straight.sort()
    relayed.sort()

    stores = [g.sync, g.scalar]
    done = [0]

    def finish(mm, i):
        mm.then_inc(T.sem["mm%d" % i], 1)
        g.vector.wait_ge(T.sem["mm%d" % i], 1)
        g.vector.tensor_copy(T.yb[0:C, C * i:C * i + C], T["ps%d" % i][0:C, 0:C]).then_inc(T.sem["cp%d" % i], 1)
        sq = stores[done[0] % 2]
        sq.wait_ge(T.sem["cp%d" % i], 1)
        sq.dma_start(T.y[:, C * i:C * i + C], T.yb[0:C, C * i:C * i + C]).then_inc(T.sem.st, 16)
        done[0] += 1

    def mult(i, t):
        return g.tensor.matmul(T["ps%d" % i][0:C, 0:C], T.xp[:, C * t:C * t + C], T["land%d" % i][:, C * t:C * t + C],
                               start=(t == 0), stop=(t == KT - 1))

    g.tensor.wait_ge(T.sem.ldp, 32)
    for _, i, q, cnt in straight:
        g.tensor.wait_ge(T.sem["arr%d" % (q % NB)], cnt)
        for t in range(KT):
            mm = mult(i, t)
        finish(mm, i)
    for _, i, q, cnt in relayed:
        g.tensor.wait_ge(T.sem["ara%d" % (q % NB)], cnt)
        mult(i, 0)
    for _, i, q, cnt in relayed:
        g.tensor.wait_ge(T.sem["arr%d" % (q % NB)], cnt)
        for t in range(1, KT):
            mm = mult(i, t)
        finish(mm, i)

    g.wait_ge(T.sem.sent, sent[0])
    g.wait_ge(T.sem.st, 16 * done[0])
